import numpy as np
import ml_dtypes


def mxq(x, axis, fmt="e4m3"):
    dtype, down = {"e4m3": (ml_dtypes.float8_e4m3fn, 7), "e5m2": (ml_dtypes.float8_e5m2, 14)}[fmt]
    v = np.moveaxis(np.asarray(x, np.float32).astype(ml_dtypes.bfloat16).astype(np.float64), axis, -1)
    blocks = v.reshape(v.shape[:-1] + (-1, 32))
    amax = np.abs(blocks).max(-1, keepdims=True)
    byte = np.maximum(np.where(amax > 0, np.frexp(amax)[1] - 1 + 127, 0) - down, 1)
    scale = np.exp2(byte - 127.0)
    codes = (blocks / scale).astype(np.float32).astype(dtype).astype(np.float64)
    return np.moveaxis((codes * scale).reshape(v.shape), -1, axis)


WIDE = False


def mx_kscale(k):
    if not WIDE:
        return np.ones(k)
    levels = np.array([10, -10, 5, -5, 0])
    if k % 512:
        return np.exp2(np.random.permutation(np.resize(levels, k // 32))).repeat(32)
    a = np.empty((k // 512, 16))
    for p in range(k // 512):
        a[p, :8] = np.random.permutation(np.resize(levels, 8))
        for g in range(8):
            far = levels[np.abs(levels - a[p, g]) >= 10]
            a[p, g + 8] = far[np.random.randint(len(far))]
    return np.exp2(a.ravel()).repeat(32)


def f64(x):
    return np.asarray(x).astype(np.float64)


def striped8(idx):
    return np.asarray(idx).reshape(8, -1, 16).transpose(0, 2, 1).reshape(128, -1).astype(np.uint16)


def unstriped8(offs):
    return offs.reshape(8, 16, -1).transpose(0, 2, 1).reshape(8, -1).astype(np.int64)


def pick8(x, idx, run):
    r = np.arange(len(x))
    return x[r[:, None], idx[r % (8 * run) // run]]


E2M1 = np.array([0.0, 0.5, 1.0, 1.5, 2.0, 3.0, 4.0, 6.0, -0.0, -0.5, -1.0, -1.5, -2.0, -3.0, -4.0, -6.0])


def pack_weight(w, fmt):
    k, n = w.shape
    w = f64(np.asarray(w, np.float32).astype(ml_dtypes.bfloat16)).reshape(k // 32, 32, n)
    amax = np.abs(w).max(1)
    if fmt == "e4m3":
        byte = np.frexp(amax)[1] - 1 + 127 - 7
    else:
        mant, ex = np.frexp(amax / 6.0)
        byte = np.where(mant > 0.5, ex, ex - 1) + 127
    byte = np.clip(np.where(amax > 0, byte, 1), 1, 254)
    scaled = (w * np.exp2(127.0 - byte)[:, None, :]).reshape(k, n).astype(np.float32)
    by_word = np.ascontiguousarray(scaled.reshape(k // 512, 128, 4, n).transpose(0, 1, 3, 2))
    if fmt == "e4m3":
        words = by_word.astype(ml_dtypes.float8_e4m3fn).view(np.uint8)
    else:
        c = by_word.astype(ml_dtypes.float4_e2m1fn).view(np.uint8) & 0xF
        words = (c[..., 0::2] | (c[..., 1::2] << 4)).reshape(k // 512, 128, 2 * n)
    return np.ascontiguousarray(words), np.ascontiguousarray(byte.astype(np.uint8).reshape(k // 512, 16, n))


def unpack_weight(words, scales, fmt):
    g, _, n = scales.shape
    words = np.ascontiguousarray(words).reshape(g, 128, n, -1)
    if fmt == "e4m3":
        vals = words.view(ml_dtypes.float8_e4m3fn).astype(np.float64)
    else:
        nib = np.empty((g, 128, n, 4), np.uint8)
        nib[..., 0::2] = words & 0xF
        nib[..., 1::2] = words >> 4
        vals = E2M1[nib]
    vals = vals * np.repeat(np.exp2(scales.astype(np.float64) - 127.0), 8, axis=1)[..., None]
    return vals.transpose(0, 1, 3, 2).reshape(g * 512, n)


D, K, T, U, X, I, Q = 512, 512, 1024, 1024, 1024, 512, 128


def setup_inputs():
    n = np.random.standard_normal
    idx = np.stack([np.random.permutation(T)[:I] for _ in range(8)])
    idx2 = np.stack([np.random.permutation(U)[:I] for _ in range(8)])
    idx3 = np.stack([np.random.permutation(X)[:I] for _ in range(8)])
    idx4 = np.stack([np.random.permutation(X)[:I] for _ in range(8)])
    idx5 = np.stack([np.random.permutation(X)[:I] for _ in range(8)])
    fd = mx_kscale(D)
    fk = mx_kscale(K)
    wqp = pack_weight(n((D, K)) * 1.0 / np.sqrt(D) * fd[:, None] * fk, "e4m3")
    cachep = pack_weight(n((K, T)) * 1.0 / np.sqrt(K) / fk[:, None], "e2m1")
    draftp = pack_weight(n((K, U)) * 1.0 / np.sqrt(K) / fk[:, None], "e4m3")
    archp = pack_weight(n((D, X)) * 1.0 / np.sqrt(D) * fd[:, None], "e2m1")
    return {
        "states": (n((D, Q)) * 0.95 / fd[:, None]).astype(np.float32),
        "wq_words": wqp[0],
        "wq_scales": wqp[1],
        "cache_words": cachep[0],
        "cache_scales": cachep[1],
        "draft_words": draftp[0],
        "draft_scales": draftp[1],
        "arch_words": archp[0],
        "arch_scales": archp[1],
        "offs": striped8(idx),
        "offs2": striped8(idx2),
        "offs3": striped8(idx3),
        "offs4": striped8(idx4),
        "offs5": striped8(idx5),
    }


def reference(states, wq_words, wq_scales, cache_words, cache_scales, draft_words, draft_scales, arch_words, arch_scales, offs, offs2, offs3, offs4, offs5):
    idx = unstriped8(offs)
    idx2 = unstriped8(offs2)
    idx3 = unstriped8(offs3)
    idx4 = unstriped8(offs4)
    idx5 = unstriped8(offs5)
    wqu = unpack_weight(wq_words, wq_scales, "e4m3")
    cacheu = unpack_weight(cache_words, cache_scales, "e2m1")
    draftu = unpack_weight(draft_words, draft_scales, "e4m3")
    archu = unpack_weight(arch_words, arch_scales, "e2m1")
    statesq = mxq(f64(states), 0, "e4m3")
    qv = wqu.T @ statesq
    qvq = mxq(qv, 0, "e4m3")
    a = qvq.T @ cacheu
    b = qvq.T @ draftu
    c0 = statesq.T @ archu
    w = np.minimum(pick8(a, idx, 16), pick8(b, idx2, 16))
    f1 = np.zeros((Q, X))
    f1[np.arange(Q)[:, None], idx3[np.arange(Q) % 128 // 16]] = w
    f2 = np.zeros((Q, X))
    f2[np.arange(Q)[:, None], idx4[np.arange(Q) % 128 // 16]] = pick8(b, idx2, 16)
    r = f1 - f2
    cc = np.maximum(c0, r)
    y = pick8(cc, idx5, 16) - w
    return y

@@ -1,0 +1,165 @@
+from contextlib import ExitStack
+
+import concourse.mybir as mybir
+
+D, K, T, I, Q = 512, 512, 1024, 512, 128
+FLOPS = 469762048
+
+F32 = mybir.dt.float32
+BF16 = mybir.dt.bfloat16
+I32 = mybir.dt.int32
+U32 = mybir.dt.uint32
+U16 = mybir.dt.uint16
+U8 = mybir.dt.uint8
+FP8X4 = mybir.dt.float8_e4m3fn_x4
+FP4X4 = mybir.dt.float4_e2m1fn_x4
+COPY = mybir.ActivationFunctionType.Copy
+ALU = mybir.AluOpType
+
+P = 128
+PACK = 4
+BANK = 512
+HALF = I // 2
+
+
+def tile_attend_handover_sidethree_kernel(tc, states, wq_words, wq_scales, cache_words, cache_scales, draft_words, draft_scales,
+                                           arch_words, arch_scales, offs, offs2, offs3, offs4, offs5, out):
+    nc = tc.nc
+    with ExitStack() as ctx:
+        keep = ctx.enter_context(tc.tile_pool(name="keep", bufs=1))
+        psum = ctx.enter_context(tc.psum_pool(name="psum", bufs=1))
+
+        def zeroed_plane(name, width):
+            plane = keep.tile([P, width], U8, name=name, align_bytes=64)
+            nc.vector.memset(plane[:].bitcast(I32), 0)
+            return plane
+
+        def load_scale_rows(queue, name, scales):
+            width = scales.shape[2]
+            rows = keep.tile([4, 4, width // 4], I32, name=name)
+            queue.dma_start(out=rows[:], in_=scales[0].bitcast(I32).rearrange("(g r) c -> r g c", r=4))
+            return rows
+
+        def spread_scale_rows(plane, rows):
+            for g in range(4):
+                nc.vector.tensor_copy(out=plane[32 * g : 32 * g + 4, :].bitcast(I32), in_=rows[:, g, :])
+
+        def load_words(name, words, nbytes):
+            tile = keep.tile([P, nbytes], U8, name=name, align_bytes=256)
+            nc.sync.dma_start(out=tile[:].bitcast(I32), in_=words.bitcast(I32))
+            return tile
+
+        def load_list(name, lists):
+            tile = keep.tile([P, I // 16], U16, name=name)
+            nc.sync.dma_start(tile[:], lists)
+            return tile
+
+        wq_plane_raw = zeroed_plane("wq_plane_raw", K)
+        arch_plane = zeroed_plane("arch_plane", T)
+        draft_plane = zeroed_plane("draft_plane", T)
+        cache_plane = zeroed_plane("cache_plane", T)
+        f2 = keep.tile([P, T], F32)
+        f1 = keep.tile([P, T], F32)
+        nc.vector.memset(f2[:], 0.0)
+        nc.vector.memset(f1[:], 0.0)
+
+        wq_rows = load_scale_rows(nc.scalar, "wq_rows", wq_scales)
+        states_raw = keep.tile([P, PACK, Q], F32, align_bytes=256)
+        nc.sync.dma_start(out=states_raw[:], in_=states.rearrange("(p t) q -> p t q", t=PACK))
+        wq_raw = load_words("wq_raw", wq_words[0].rearrange("p n t -> p (n t)"), 4 * K)
+        arch_rows = load_scale_rows(nc.sync, "arch_rows", arch_scales)
+        arch_sb = load_words("arch_sb", arch_words[0], 2 * T)
+        draft_rows = load_scale_rows(nc.sync, "draft_rows", draft_scales)
+        draft_sb = load_words("draft_sb", draft_words[0].rearrange("p n t -> p (n t)"), 4 * T)
+        cache_rows = load_scale_rows(nc.sync, "cache_rows", cache_scales)
+        cache_sb = load_words("cache_sb", cache_words[0], 2 * T)
+        list2 = load_list("list2", offs2)
+        list4 = load_list("list4", offs4)
+        list1 = load_list("list1", offs)
+        list3 = load_list("list3", offs3)
+        list5 = load_list("list5", offs5)
+
+        spread_scale_rows(wq_plane_raw, wq_rows)
+        wq_plane = keep.tile([P, K], U8, align_bytes=64)
+        nc.vector.tensor_copy(out=wq_plane[:].rearrange("p (t m) -> p m t", t=PACK), in_=wq_plane_raw[:].rearrange("p (m t) -> p m t", t=PACK))
+
+        states_bf = keep.tile([P, Q, PACK], BF16, align_bytes=64)
+        nc.vector.tensor_copy(out=states_bf[:], in_=states_raw[:].rearrange("p t q -> p q t"))
+        s_codes = keep.tile([P, Q], U32, align_bytes=64)
+        s_plane = keep.tile([P, Q], U8, align_bytes=64)
+        nc.vector.quantize_mx(out=s_codes[:].bitcast(FP8X4), scales=s_plane[:], in_=states_bf[:].rearrange("p q t -> p (q t)"))
+
+        wq_sb = keep.tile([P, K], U32, align_bytes=64)
+        nc.scalar.copy(out=wq_sb[:].rearrange("p (t m) -> p m t", t=PACK), in_=wq_raw[:].bitcast(U32).rearrange("p (m t) -> p m t", t=PACK))
+
+        qv_ps = psum.tile([P, BANK], F32, tag="first")
+        for t in range(PACK):
+            cols = slice(t * P, (t + 1) * P)
+            nc.tensor.matmul_mx(out=qv_ps[:, cols], lhsT=wq_sb[:, cols].bitcast(FP8X4), lhsT_scale=wq_plane[:, cols],
+                                rhs=s_codes[:].bitcast(FP8X4), rhs_scale=s_plane[:], start=True, stop=True)
+        qv_bf = keep.tile([P, Q, PACK], BF16, align_bytes=64)
+        nc.scalar.copy(out=qv_bf[:], in_=qv_ps[:].rearrange("p (t q) -> p q t", t=PACK))
+
+        spread_scale_rows(arch_plane, arch_rows)
+        c0_ps = []
+        for h in range(2):
+            bank = psum.tile([P, BANK], F32, name="c0_%d" % h)
+            nc.tensor.matmul_mx(out=bank[:], lhsT=s_codes[:].bitcast(FP8X4), lhsT_scale=s_plane[:],
+                                rhs=arch_sb[:, 2 * BANK * h : 2 * BANK * (h + 1)].bitcast(FP4X4), rhs_scale=arch_plane[:, BANK * h : BANK * (h + 1)],
+                                start=True, stop=True)
+            c0_ps.append(bank)
+
+        spread_scale_rows(draft_plane, draft_rows)
+        q_codes = keep.tile([P, Q], U32, align_bytes=64)
+        q_plane = keep.tile([P, Q], U8, align_bytes=64)
+        nc.vector.quantize_mx(out=q_codes[:].bitcast(FP8X4), scales=q_plane[:], in_=qv_bf[:].rearrange("p q t -> p (q t)"))
+        spread_scale_rows(cache_plane, cache_rows)
+
+        b_sb = keep.tile([P, T], F32)
+        lo = 0
+        for j, width in enumerate((512, 256, 128, 128)):
+            bank = psum.tile([P, BANK], F32, name="b_%d" % j, tag="first" if j == 3 else "b_%d" % j)
+            nc.tensor.matmul_mx(out=bank[:, :width], lhsT=q_codes[:].bitcast(FP8X4), lhsT_scale=q_plane[:],
+                                rhs=draft_sb[:, 4 * lo : 4 * (lo + width)].bitcast(FP8X4), rhs_scale=draft_plane[:, lo : lo + width],
+                                start=True, stop=True)
+            if j % 2 == 0:
+                nc.scalar.copy(out=b_sb[:, lo : lo + width], in_=bank[:, :width])
+            else:
+                nc.vector.tensor_copy(out=b_sb[:, lo : lo + width], in_=bank[:, :width])
+            lo = lo + width
+
+        gb = keep.tile([P, I], F32)
+        nc.vector.tensor_copy(gb[:, :HALF], b_sb[:].indirect(list2[:, : HALF // 16]))
+        nc.scalar.activation(gb[:, HALF:], b_sb[:].indirect(list2[:, HALF // 16 :]), COPY)
+        nc.scalar.activation(f2[:].indirect(list4[:]), gb[:], COPY)
+
+        a_sb = keep.tile([P, T], F32)
+        for h in range(2):
+            bank = psum.tile([P, BANK], F32, name="a_%d" % h)
+            nc.tensor.matmul_mx(out=bank[:], lhsT=q_codes[:].bitcast(FP8X4), lhsT_scale=q_plane[:],
+                                rhs=cache_sb[:, 2 * BANK * h : 2 * BANK * (h + 1)].bitcast(FP4X4), rhs_scale=cache_plane[:, BANK * h : BANK * (h + 1)],
+                                start=True, stop=True)
+            nc.vector.tensor_copy(out=a_sb[:, BANK * h : BANK * (h + 1)], in_=bank[:])
+        ga = keep.tile([P, I], F32)
+        nc.vector.tensor_copy(ga[:], a_sb[:].indirect(list1[:]))
+        w = keep.tile([P, I], F32)
+        nc.vector.tensor_tensor(w[:], ga[:], gb[:], ALU.min)
+        nc.scalar.activation(f1[:].indirect(list3[:]), w[:], COPY)
+
+        r = keep.tile([P, T], F32)
+        cc = keep.tile([P, T], F32)
+        for h in range(2):
+            cols = slice(BANK * h, BANK * (h + 1))
+            nc.vector.tensor_tensor(r[:, cols], f1[:, cols], f2[:, cols], ALU.subtract)
+        for h in range(2):
+            cols = slice(BANK * h, BANK * (h + 1))
+            nc.vector.tensor_tensor(cc[:, cols], c0_ps[h][:], r[:, cols], ALU.max)
+
+        y0 = keep.tile([P, HALF], F32, align_bytes=256)
+        y1 = keep.tile([P, HALF], F32, align_bytes=256)
+        gc = keep.tile([P, HALF], F32)
+        nc.vector.tensor_tensor(y0[:], cc[:].indirect(list5[:, : HALF // 16]), w[:, :HALF], ALU.subtract)
+        nc.scalar.activation(gc[:], cc[:].indirect(list5[:, HALF // 16 :]), COPY)
+        nc.sync.dma_start(out=out[:, :HALF], in_=y0[:])
+        nc.vector.tensor_tensor(y1[:], gc[:], w[:, HALF:], ALU.subtract)
+        nc.scalar.dma_start(out=out[:, HALF:], in_=y1[:])

@@ -34,18 +34,28 @@ def tile_attend_handover_sidethree_kernel(tc, states, wq_words, wq_scales, cache
             nc.vector.memset(plane[:].bitcast(I32), 0)
             return plane
 
-        def load_scale_rows(queue, name, scales):
-            width = scales.shape[2]
-            rows = keep.tile([4, 4, width // 4], I32, name=name)
-            queue.dma_start(out=rows[:], in_=scales[0].bitcast(I32).rearrange("(g r) c -> r g c", r=4))
-            return rows
-
-        def spread_scale_rows(plane, rows):
+        def load_plane(plane, scales):
             for g in range(4):
-                nc.vector.tensor_copy(out=plane[32 * g : 32 * g + 4, :].bitcast(I32), in_=rows[:, g, :])
+                nc.sync.dma_start(out=plane[32 * g : 32 * g + 4, :].bitcast(I32), in_=scales[0, 4 * g : 4 * g + 4, :].bitcast(I32))
 
-        def load_words(name, words, nbytes):
-            tile = keep.tile([P, nbytes], U8, name=name, align_bytes=256)
+        def zeroed_half(name, width, home):
+            plane = keep.tile([P, 2, width // 4], I32, name=name, align_bytes=64)
+            nc.vector.memset(plane[home : home + 64], 0)
+            return plane
+
+        def load_half(plane, scales, home):
+            rows = scales[0].bitcast(I32).rearrange("(h g r) c -> g r h c", h=2, g=2)
+            for g in range(2):
+                nc.scalar.dma_start(out=plane[home + 32 * g : home + 32 * g + 4], in_=rows[g])
+
+        def finish_half(plane, home):
+            own = home // 64
+            away = 64 - home
+            nc.vector.tensor_copy(out=plane[away : away + 64, own, :], in_=plane[home : home + 64, 1 - own, :])
+            return plane[:, own, :].bitcast(U8)
+
+        def load_words(name, words, nbytes, tag=None):
+            tile = keep.tile([P, nbytes], U8, name=name, tag=tag or name, align_bytes=256)
             nc.sync.dma_start(out=tile[:].bitcast(I32), in_=words.bitcast(I32))
             return tile
 
@@ -54,68 +64,62 @@ def tile_attend_handover_sidethree_kernel(tc, states, wq_words, wq_scales, cache
             nc.sync.dma_start(tile[:], lists)
             return tile
 
-        wq_plane_raw = zeroed_plane("wq_plane_raw", K)
-        arch_plane = zeroed_plane("arch_plane", T)
-        draft_plane = zeroed_plane("draft_plane", T)
+        wq_half = zeroed_half("wq_half", K, 0)
+        draft_half = zeroed_half("draft_half", T, 64)
         cache_plane = zeroed_plane("cache_plane", T)
-        f2 = keep.tile([P, T], F32)
-        f1 = keep.tile([P, T], F32)
-        nc.vector.memset(f2[:], 0.0)
-        nc.vector.memset(f1[:], 0.0)
+        arch_plane = zeroed_plane("arch_plane", T)
 
-        wq_rows = load_scale_rows(nc.scalar, "wq_rows", wq_scales)
+        load_half(wq_half, wq_scales, 0)
+        load_half(draft_half, draft_scales, 64)
         states_raw = keep.tile([P, PACK, Q], F32, align_bytes=256)
         nc.sync.dma_start(out=states_raw[:], in_=states.rearrange("(p t) q -> p t q", t=PACK))
-        wq_raw = load_words("wq_raw", wq_words[0].rearrange("p n t -> p (n t)"), 4 * K)
-        arch_rows = load_scale_rows(nc.sync, "arch_rows", arch_scales)
-        arch_sb = load_words("arch_sb", arch_words[0], 2 * T)
-        draft_rows = load_scale_rows(nc.sync, "draft_rows", draft_scales)
+        wq_raw = load_words("wq_raw", wq_words[0].rearrange("p n t -> p (n t)"), 4 * K, "then_f2")
         draft_sb = load_words("draft_sb", draft_words[0].rearrange("p n t -> p (n t)"), 4 * T)
-        cache_rows = load_scale_rows(nc.sync, "cache_rows", cache_scales)
-        cache_sb = load_words("cache_sb", cache_words[0], 2 * T)
         list2 = load_list("list2", offs2)
+        cache_sb = load_words("cache_sb", cache_words[0], 2 * T)
+        load_plane(cache_plane, cache_scales)
         list4 = load_list("list4", offs4)
         list1 = load_list("list1", offs)
         list3 = load_list("list3", offs3)
+        arch_sb = load_words("arch_sb", arch_words[0], 2 * T)
+        load_plane(arch_plane, arch_scales)
         list5 = load_list("list5", offs5)
 
-        spread_scale_rows(wq_plane_raw, wq_rows)
-        wq_plane = keep.tile([P, K], U8, align_bytes=64)
-        nc.vector.tensor_copy(out=wq_plane[:].rearrange("p (t m) -> p m t", t=PACK), in_=wq_plane_raw[:].rearrange("p (m t) -> p m t", t=PACK))
-
+        wq_plane_raw = finish_half(wq_half, 0)
         states_bf = keep.tile([P, Q, PACK], BF16, align_bytes=64)
         nc.vector.tensor_copy(out=states_bf[:], in_=states_raw[:].rearrange("p t q -> p q t"))
+        wq_plane = keep.tile([P, K], U8, align_bytes=64)
+        nc.vector.tensor_copy(out=wq_plane[:].rearrange("p (t m) -> p m t", t=PACK), in_=wq_plane_raw.rearrange("p (m t) -> p m t", t=PACK))
         s_codes = keep.tile([P, Q], U32, align_bytes=64)
         s_plane = keep.tile([P, Q], U8, align_bytes=64)
         nc.vector.quantize_mx(out=s_codes[:].bitcast(FP8X4), scales=s_plane[:], in_=states_bf[:].rearrange("p q t -> p (q t)"))
 
         wq_sb = keep.tile([P, K], U32, align_bytes=64)
-        nc.scalar.copy(out=wq_sb[:].rearrange("p (t m) -> p m t", t=PACK), in_=wq_raw[:].bitcast(U32).rearrange("p (m t) -> p m t", t=PACK))
+        dealt = wq_sb[:].rearrange("p (t m) -> p m t", t=PACK)
+        natural = wq_raw[:].bitcast(U32).rearrange("p (m t) -> p m t", t=PACK)
+        nc.scalar.copy(out=dealt[:, :64, :], in_=natural[:, :64, :])
+        dealt_i = wq_sb[:].bitcast(I32).rearrange("p (t m) -> p m t", t=PACK)
+        natural_i = wq_raw[:].bitcast(I32).rearrange("p (m t) -> p m t", t=PACK)
+        nc.vector.tensor_copy(out=dealt_i[:, 64:, :], in_=natural_i[:, 64:, :])
+        draft_plane = finish_half(draft_half, 64)
 
+        f2 = keep.tile([P, T], F32, tag="then_f2", align_bytes=256)
+        nc.vector.memset(f2[:], 0.0)
         qv_ps = psum.tile([P, BANK], F32, tag="first")
         for t in range(PACK):
             cols = slice(t * P, (t + 1) * P)
             nc.tensor.matmul_mx(out=qv_ps[:, cols], lhsT=wq_sb[:, cols].bitcast(FP8X4), lhsT_scale=wq_plane[:, cols],
                                 rhs=s_codes[:].bitcast(FP8X4), rhs_scale=s_plane[:], start=True, stop=True)
-        qv_bf = keep.tile([P, Q, PACK], BF16, align_bytes=64)
+        qv_bf = keep.tile([P, Q, PACK], BF16, tag="then_f1", align_bytes=64)
         nc.scalar.copy(out=qv_bf[:], in_=qv_ps[:].rearrange("p (t q) -> p q t", t=PACK))
 
-        spread_scale_rows(arch_plane, arch_rows)
-        c0_ps = []
-        for h in range(2):
-            bank = psum.tile([P, BANK], F32, name="c0_%d" % h)
-            nc.tensor.matmul_mx(out=bank[:], lhsT=s_codes[:].bitcast(FP8X4), lhsT_scale=s_plane[:],
-                                rhs=arch_sb[:, 2 * BANK * h : 2 * BANK * (h + 1)].bitcast(FP4X4), rhs_scale=arch_plane[:, BANK * h : BANK * (h + 1)],
-                                start=True, stop=True)
-            c0_ps.append(bank)
-
-        spread_scale_rows(draft_plane, draft_rows)
         q_codes = keep.tile([P, Q], U32, align_bytes=64)
         q_plane = keep.tile([P, Q], U8, align_bytes=64)
         nc.vector.quantize_mx(out=q_codes[:].bitcast(FP8X4), scales=q_plane[:], in_=qv_bf[:].rearrange("p q t -> p (q t)"))
-        spread_scale_rows(cache_plane, cache_rows)
 
-        b_sb = keep.tile([P, T], F32)
+        f1 = keep.tile([P, T], F32, tag="then_f1", align_bytes=64)
+        nc.vector.memset(f1[:], 0.0)
+        b_sb = keep.tile([P, T], F32, tag="scores")
         lo = 0
         for j, width in enumerate((512, 256, 128, 128)):
             bank = psum.tile([P, BANK], F32, name="b_%d" % j, tag="first" if j == 3 else "b_%d" % j)
@@ -133,7 +137,7 @@ def tile_attend_handover_sidethree_kernel(tc, states, wq_words, wq_scales, cache
         nc.scalar.activation(gb[:, HALF:], b_sb[:].indirect(list2[:, HALF // 16 :]), COPY)
         nc.scalar.activation(f2[:].indirect(list4[:]), gb[:], COPY)
 
-        a_sb = keep.tile([P, T], F32)
+        a_sb = keep.tile([P, T], F32, tag="scores")
         for h in range(2):
             bank = psum.tile([P, BANK], F32, name="a_%d" % h)
             nc.tensor.matmul_mx(out=bank[:], lhsT=q_codes[:].bitcast(FP8X4), lhsT_scale=q_plane[:],
@@ -141,10 +145,21 @@ def tile_attend_handover_sidethree_kernel(tc, states, wq_words, wq_scales, cache
                                 start=True, stop=True)
             nc.vector.tensor_copy(out=a_sb[:, BANK * h : BANK * (h + 1)], in_=bank[:])
         ga = keep.tile([P, I], F32)
-        nc.vector.tensor_copy(ga[:], a_sb[:].indirect(list1[:]))
         w = keep.tile([P, I], F32)
-        nc.vector.tensor_tensor(w[:], ga[:], gb[:], ALU.min)
+        for h in range(2):
+            nc.vector.tensor_copy(ga[:, HALF * h : HALF * (h + 1)], a_sb[:].indirect(list1[:, HALF // 16 * h : HALF // 16 * (h + 1)]))
+        for h in range(2):
+            cols = slice(HALF * h, HALF * (h + 1))
+            nc.vector.tensor_tensor(w[:, cols], ga[:, cols], gb[:, cols], ALU.min)
         nc.scalar.activation(f1[:].indirect(list3[:]), w[:], COPY)
+
+        c0_ps = []
+        for h in range(2):
+            bank = psum.tile([P, BANK], F32, name="c0_%d" % h, tag="b_%d" % h)
+            nc.tensor.matmul_mx(out=bank[:], lhsT=s_codes[:].bitcast(FP8X4), lhsT_scale=s_plane[:],
+                                rhs=arch_sb[:, 2 * BANK * h : 2 * BANK * (h + 1)].bitcast(FP4X4), rhs_scale=arch_plane[:, BANK * h : BANK * (h + 1)],
+                                start=True, stop=True)
+            c0_ps.append(bank)
 
         r = keep.tile([P, T], F32)
         cc = keep.tile([P, T], F32)

@@ -34,25 +34,9 @@ def tile_attend_handover_sidethree_kernel(tc, states, wq_words, wq_scales, cache
             nc.vector.memset(plane[:].bitcast(I32), 0)
             return plane
 
-        def load_plane(plane, scales):
+        def load_plane(queue, plane, scales):
             for g in range(4):
-                nc.sync.dma_start(out=plane[32 * g : 32 * g + 4, :].bitcast(I32), in_=scales[0, 4 * g : 4 * g + 4, :].bitcast(I32))
-
-        def zeroed_half(name, width, home):
-            plane = keep.tile([P, 2, width // 4], I32, name=name, align_bytes=64)
-            nc.vector.memset(plane[home : home + 64], 0)
-            return plane
-
-        def load_half(plane, scales, home):
-            rows = scales[0].bitcast(I32).rearrange("(h g r) c -> g r h c", h=2, g=2)
-            for g in range(2):
-                nc.scalar.dma_start(out=plane[home + 32 * g : home + 32 * g + 4], in_=rows[g])
-
-        def finish_half(plane, home):
-            own = home // 64
-            away = 64 - home
-            nc.vector.tensor_copy(out=plane[away : away + 64, own, :], in_=plane[home : home + 64, 1 - own, :])
-            return plane[:, own, :].bitcast(U8)
+                queue.dma_start(out=plane[32 * g : 32 * g + 4, :].bitcast(I32), in_=scales[0, 4 * g : 4 * g + 4, :].bitcast(I32))
 
         def load_words(name, words, nbytes, tag=None):
             tile = keep.tile([P, nbytes], U8, name=name, tag=tag or name, align_bytes=256)
@@ -64,32 +48,33 @@ def tile_attend_handover_sidethree_kernel(tc, states, wq_words, wq_scales, cache
             nc.sync.dma_start(tile[:], lists)
             return tile
 
-        wq_half = zeroed_half("wq_half", K, 0)
-        draft_half = zeroed_half("draft_half", T, 64)
+        wq_plane_raw = zeroed_plane("wq_plane_raw", K)
+        draft_plane = zeroed_plane("draft_plane", T)
         cache_plane = zeroed_plane("cache_plane", T)
         arch_plane = zeroed_plane("arch_plane", T)
+        f2 = keep.tile([P, T], F32)
+        nc.vector.memset(f2[:], 0.0)
 
-        load_half(wq_half, wq_scales, 0)
-        load_half(draft_half, draft_scales, 64)
         states_raw = keep.tile([P, PACK, Q], F32, align_bytes=256)
         nc.sync.dma_start(out=states_raw[:], in_=states.rearrange("(p t) q -> p t q", t=PACK))
-        wq_raw = load_words("wq_raw", wq_words[0].rearrange("p n t -> p (n t)"), 4 * K, "then_f2")
-        draft_sb = load_words("draft_sb", draft_words[0].rearrange("p n t -> p (n t)"), 4 * T)
+        load_plane(nc.scalar, wq_plane_raw, wq_scales)
+        wq_raw = load_words("wq_raw", wq_words[0].rearrange("p n t -> p (n t)"), 4 * K)
         list2 = load_list("list2", offs2)
-        cache_sb = load_words("cache_sb", cache_words[0], 2 * T)
-        load_plane(cache_plane, cache_scales)
         list4 = load_list("list4", offs4)
+        draft_sb = load_words("draft_sb", draft_words[0].rearrange("p n t -> p (n t)"), 4 * T)
+        load_plane(nc.sync, draft_plane, draft_scales)
+        cache_sb = load_words("cache_sb", cache_words[0], 2 * T)
+        load_plane(nc.sync, cache_plane, cache_scales)
         list1 = load_list("list1", offs)
         list3 = load_list("list3", offs3)
         arch_sb = load_words("arch_sb", arch_words[0], 2 * T)
-        load_plane(arch_plane, arch_scales)
+        load_plane(nc.sync, arch_plane, arch_scales)
         list5 = load_list("list5", offs5)
 
-        wq_plane_raw = finish_half(wq_half, 0)
         states_bf = keep.tile([P, Q, PACK], BF16, align_bytes=64)
         nc.vector.tensor_copy(out=states_bf[:], in_=states_raw[:].rearrange("p t q -> p q t"))
         wq_plane = keep.tile([P, K], U8, align_bytes=64)
-        nc.vector.tensor_copy(out=wq_plane[:].rearrange("p (t m) -> p m t", t=PACK), in_=wq_plane_raw.rearrange("p (m t) -> p m t", t=PACK))
+        nc.vector.tensor_copy(out=wq_plane[:].rearrange("p (t m) -> p t m", t=PACK), in_=wq_plane_raw[:].rearrange("p (m t) -> p t m", t=PACK))
         s_codes = keep.tile([P, Q], U32, align_bytes=64)
         s_plane = keep.tile([P, Q], U8, align_bytes=64)
         nc.vector.quantize_mx(out=s_codes[:].bitcast(FP8X4), scales=s_plane[:], in_=states_bf[:].rearrange("p q t -> p (q t)"))
@@ -97,21 +82,16 @@ def tile_attend_handover_sidethree_kernel(tc, states, wq_words, wq_scales, cache
         wq_sb = keep.tile([P, K], U32, align_bytes=64)
         dealt = wq_sb[:].rearrange("p (t m) -> p m t", t=PACK)
         natural = wq_raw[:].bitcast(U32).rearrange("p (m t) -> p m t", t=PACK)
-        nc.scalar.copy(out=dealt[:, :64, :], in_=natural[:, :64, :])
-        dealt_i = wq_sb[:].bitcast(I32).rearrange("p (t m) -> p m t", t=PACK)
-        natural_i = wq_raw[:].bitcast(I32).rearrange("p (m t) -> p m t", t=PACK)
-        nc.vector.tensor_copy(out=dealt_i[:, 64:, :], in_=natural_i[:, 64:, :])
-        draft_plane = finish_half(draft_half, 64)
+        nc.scalar.copy(out=dealt, in_=natural)
 
-        f2 = keep.tile([P, T], F32, tag="then_f2", align_bytes=256)
-        nc.vector.memset(f2[:], 0.0)
-        qv_ps = psum.tile([P, BANK], F32, tag="first")
+        qv_ps = [psum.tile([P, BANK], F32, name="qv_%d" % h, tag="first_%d" % h) for h in range(2)]
         for t in range(PACK):
             cols = slice(t * P, (t + 1) * P)
-            nc.tensor.matmul_mx(out=qv_ps[:, cols], lhsT=wq_sb[:, cols].bitcast(FP8X4), lhsT_scale=wq_plane[:, cols],
+            nc.tensor.matmul_mx(out=qv_ps[t // 2][:, t % 2 * Q : (t % 2 + 1) * Q], lhsT=wq_sb[:, cols].bitcast(FP8X4), lhsT_scale=wq_plane[:, cols],
                                 rhs=s_codes[:].bitcast(FP8X4), rhs_scale=s_plane[:], start=True, stop=True)
         qv_bf = keep.tile([P, Q, PACK], BF16, tag="then_f1", align_bytes=64)
-        nc.scalar.copy(out=qv_bf[:], in_=qv_ps[:].rearrange("p (t q) -> p q t", t=PACK))
+        nc.vector.tensor_copy(out=qv_bf[:, :, 0:2], in_=qv_ps[0][:, : 2 * Q].rearrange("p (t q) -> p q t", t=2))
+        nc.scalar.copy(out=qv_bf[:, :, 2:4], in_=qv_ps[1][:, : 2 * Q].rearrange("p (t q) -> p q t", t=2))
 
         q_codes = keep.tile([P, Q], U32, align_bytes=64)
         q_plane = keep.tile([P, Q], U8, align_bytes=64)
@@ -122,7 +102,7 @@ def tile_attend_handover_sidethree_kernel(tc, states, wq_words, wq_scales, cache
         b_sb = keep.tile([P, T], F32, tag="scores")
         lo = 0
         for j, width in enumerate((512, 256, 128, 128)):
-            bank = psum.tile([P, BANK], F32, name="b_%d" % j, tag="first" if j == 3 else "b_%d" % j)
+            bank = psum.tile([P, BANK], F32, name="b_%d" % j, tag="b_%d" % j)
             nc.tensor.matmul_mx(out=bank[:, :width], lhsT=q_codes[:].bitcast(FP8X4), lhsT_scale=q_plane[:],
                                 rhs=draft_sb[:, 4 * lo : 4 * (lo + width)].bitcast(FP8X4), rhs_scale=draft_plane[:, lo : lo + width],
                                 start=True, stop=True)
@@ -139,19 +119,24 @@ def tile_attend_handover_sidethree_kernel(tc, states, wq_words, wq_scales, cache
 
         a_sb = keep.tile([P, T], F32, tag="scores")
         for h in range(2):
-            bank = psum.tile([P, BANK], F32, name="a_%d" % h)
+            bank = psum.tile([P, BANK], F32, name="a_%d" % h, tag="first_%d" % h)
             nc.tensor.matmul_mx(out=bank[:], lhsT=q_codes[:].bitcast(FP8X4), lhsT_scale=q_plane[:],
                                 rhs=cache_sb[:, 2 * BANK * h : 2 * BANK * (h + 1)].bitcast(FP4X4), rhs_scale=cache_plane[:, BANK * h : BANK * (h + 1)],
                                 start=True, stop=True)
             nc.vector.tensor_copy(out=a_sb[:, BANK * h : BANK * (h + 1)], in_=bank[:])
-        ga = keep.tile([P, I], F32)
+        ga = keep.tile([P, I], F32, tag="then_late")
         w = keep.tile([P, I], F32)
         for h in range(2):
             nc.vector.tensor_copy(ga[:, HALF * h : HALF * (h + 1)], a_sb[:].indirect(list1[:, HALF // 16 * h : HALF // 16 * (h + 1)]))
         for h in range(2):
             cols = slice(HALF * h, HALF * (h + 1))
             nc.vector.tensor_tensor(w[:, cols], ga[:, cols], gb[:, cols], ALU.min)
-        nc.scalar.activation(f1[:].indirect(list3[:]), w[:], COPY)
+        f1_late = keep.tile([P, T], F32, tag="then_late")
+        nc.vector.memset(f1_late[:], 0.0)
+        nc.scalar.activation(f1[:].indirect(list3[:, : HALF // 16]), w[:, :HALF], COPY)
+        nc.scalar.activation(f1_late[:].indirect(list3[:, HALF // 16 :]), w[:, HALF:], COPY)
+        r_early = keep.tile([P, T], F32)
+        nc.vector.tensor_tensor(r_early[:], f1[:], f2[:], ALU.subtract)
 
         c0_ps = []
         for h in range(2):
@@ -165,7 +150,7 @@ def tile_attend_handover_sidethree_kernel(tc, states, wq_words, wq_scales, cache
         cc = keep.tile([P, T], F32)
         for h in range(2):
             cols = slice(BANK * h, BANK * (h + 1))
-            nc.vector.tensor_tensor(r[:, cols], f1[:, cols], f2[:, cols], ALU.subtract)
+            nc.vector.tensor_tensor(r[:, cols], f1_late[:, cols], r_early[:, cols], ALU.add)
         for h in range(2):
             cols = slice(BANK * h, BANK * (h + 1))
             nc.vector.tensor_tensor(cc[:, cols], c0_ps[h][:], r[:, cols], ALU.max)

@@ -74,15 +74,18 @@ def tile_attend_handover_sidethree_kernel(tc, states, wq_words, wq_scales, cache
         states_bf = keep.tile([P, Q, PACK], BF16, align_bytes=64)
         nc.vector.tensor_copy(out=states_bf[:], in_=states_raw[:].rearrange("p t q -> p q t"))
         wq_plane = keep.tile([P, K], U8, align_bytes=64)
-        nc.vector.tensor_copy(out=wq_plane[:].rearrange("p (t m) -> p t m", t=PACK), in_=wq_plane_raw[:].rearrange("p (m t) -> p t m", t=PACK))
         s_codes = keep.tile([P, Q], U32, align_bytes=64)
         s_plane = keep.tile([P, Q], U8, align_bytes=64)
         nc.vector.quantize_mx(out=s_codes[:].bitcast(FP8X4), scales=s_plane[:], in_=states_bf[:].rearrange("p q t -> p (q t)"))
 
+        for h in range(2):
+            nc.vector.tensor_copy(out=wq_plane[:].rearrange("p (t m) -> p t m", t=PACK)[:, 2 * h : 2 * h + 2, :],
+                                  in_=wq_plane_raw[:].rearrange("p (m t) -> p t m", t=PACK)[:, 2 * h : 2 * h + 2, :])
         wq_sb = keep.tile([P, K], U32, align_bytes=64)
         dealt = wq_sb[:].rearrange("p (t m) -> p m t", t=PACK)
         natural = wq_raw[:].bitcast(U32).rearrange("p (m t) -> p m t", t=PACK)
-        nc.scalar.copy(out=dealt, in_=natural)
+        for h in range(2):
+            nc.scalar.copy(out=dealt[:, :, 2 * h : 2 * h + 2], in_=natural[:, :, 2 * h : 2 * h + 2])
 
         qv_ps = [psum.tile([P, BANK], F32, name="qv_%d" % h, tag="first_%d" % h) for h in range(2)]
         for t in range(PACK):
@@ -161,5 +164,7 @@ def tile_attend_handover_sidethree_kernel(tc, states, wq_words, wq_scales, cache
         nc.vector.tensor_tensor(y0[:], cc[:].indirect(list5[:, : HALF // 16]), w[:, :HALF], ALU.subtract)
         nc.scalar.activation(gc[:], cc[:].indirect(list5[:, HALF // 16 :]), COPY)
         nc.sync.dma_start(out=out[:, :HALF], in_=y0[:])
-        nc.vector.tensor_tensor(y1[:], gc[:], w[:, HALF:], ALU.subtract)
-        nc.scalar.dma_start(out=out[:, HALF:], in_=y1[:])
+        for j, queue in enumerate((nc.scalar, nc.sync)):
+            cols = slice(HALF // 2 * j, HALF // 2 * (j + 1))
+            nc.vector.tensor_tensor(y1[:, cols], gc[:, cols], w[:, HALF:][:, cols], ALU.subtract)
+            queue.dma_start(out=out[:, HALF:][:, cols], in_=y1[:, cols])

from contextlib import ExitStack

import concourse.mybir as mybir

D, K, T, I, Q = 512, 512, 1024, 512, 128
FLOPS = 469762048

F32 = mybir.dt.float32
BF16 = mybir.dt.bfloat16
I32 = mybir.dt.int32
U32 = mybir.dt.uint32
U16 = mybir.dt.uint16
U8 = mybir.dt.uint8
FP8X4 = mybir.dt.float8_e4m3fn_x4
FP4X4 = mybir.dt.float4_e2m1fn_x4
COPY = mybir.ActivationFunctionType.Copy
ALU = mybir.AluOpType

P = 128
PACK = 4
BANK = 512
HALF = I // 2


def tile_attend_handover_sidethree_kernel(tc, states, wq_words, wq_scales, cache_words, cache_scales, draft_words, draft_scales,
                                           arch_words, arch_scales, offs, offs2, offs3, offs4, offs5, out):
    nc = tc.nc
    with ExitStack() as ctx:
        keep = ctx.enter_context(tc.tile_pool(name="keep", bufs=1))
        psum = ctx.enter_context(tc.psum_pool(name="psum", bufs=1))

        def zeroed_plane(name, width):
            plane = keep.tile([P, width], U8, name=name, align_bytes=64)
            nc.vector.memset(plane[:].bitcast(I32), 0)
            return plane

        def load_plane(queue, plane, scales):
            for g in range(4):
                queue.dma_start(out=plane[32 * g : 32 * g + 4, :].bitcast(I32), in_=scales[0, 4 * g : 4 * g + 4, :].bitcast(I32))

        def load_words(name, words, nbytes, tag=None):
            tile = keep.tile([P, nbytes], U8, name=name, tag=tag or name, align_bytes=256)
            nc.sync.dma_start(out=tile[:].bitcast(I32), in_=words.bitcast(I32))
            return tile

        def load_list(name, lists):
            tile = keep.tile([P, I // 16], U16, name=name)
            nc.sync.dma_start(tile[:], lists)
            return tile

        wq_plane_raw = zeroed_plane("wq_plane_raw", K)
        draft_plane = zeroed_plane("draft_plane", T)
        cache_plane = zeroed_plane("cache_plane", T)
        arch_plane = zeroed_plane("arch_plane", T)
        f2 = keep.tile([P, T], F32)
        nc.vector.memset(f2[:], 0.0)

        states_raw = keep.tile([P, PACK, Q], F32, align_bytes=256)
        nc.sync.dma_start(out=states_raw[:], in_=states.rearrange("(p t) q -> p t q", t=PACK))
        load_plane(nc.scalar, wq_plane_raw, wq_scales)
        wq_raw = load_words("wq_raw", wq_words[0].rearrange("p n t -> p (n t)"), 4 * K)
        list2 = load_list("list2", offs2)
        list4 = load_list("list4", offs4)
        draft_sb = load_words("draft_sb", draft_words[0].rearrange("p n t -> p (n t)"), 4 * T)
        load_plane(nc.sync, draft_plane, draft_scales)
        cache_sb = load_words("cache_sb", cache_words[0], 2 * T)
        load_plane(nc.sync, cache_plane, cache_scales)
        list1 = load_list("list1", offs)
        list3 = load_list("list3", offs3)
        arch_sb = load_words("arch_sb", arch_words[0], 2 * T)
        load_plane(nc.sync, arch_plane, arch_scales)
        list5 = load_list("list5", offs5)

        states_bf = keep.tile([P, Q, PACK], BF16, align_bytes=64)
        nc.vector.tensor_copy(out=states_bf[:], in_=states_raw[:].rearrange("p t q -> p q t"))
        wq_plane = keep.tile([P, K], U8, align_bytes=64)
        s_codes = keep.tile([P, Q], U32, align_bytes=64)
        s_plane = keep.tile([P, Q], U8, align_bytes=64)
        nc.vector.quantize_mx(out=s_codes[:].bitcast(FP8X4), scales=s_plane[:], in_=states_bf[:].rearrange("p q t -> p (q t)"))

        for h in range(2):
            nc.vector.tensor_copy(out=wq_plane[:].rearrange("p (t m) -> p t m", t=PACK)[:, 2 * h : 2 * h + 2, :],
                                  in_=wq_plane_raw[:].rearrange("p (m t) -> p t m", t=PACK)[:, 2 * h : 2 * h + 2, :])
        wq_sb = keep.tile([P, K], U32, align_bytes=64)
        dealt = wq_sb[:].rearrange("p (t m) -> p m t", t=PACK)
        natural = wq_raw[:].bitcast(U32).rearrange("p (m t) -> p m t", t=PACK)
        for h in range(2):
            nc.scalar.copy(out=dealt[:, :, 2 * h : 2 * h + 2], in_=natural[:, :, 2 * h : 2 * h + 2])

        qv_ps = [psum.tile([P, BANK], F32, name="qv_%d" % h, tag="first_%d" % h) for h in range(2)]
        for t in range(PACK):
            cols = slice(t * P, (t + 1) * P)
            nc.tensor.matmul_mx(out=qv_ps[t // 2][:, t % 2 * Q : (t % 2 + 1) * Q], lhsT=wq_sb[:, cols].bitcast(FP8X4), lhsT_scale=wq_plane[:, cols],
                                rhs=s_codes[:].bitcast(FP8X4), rhs_scale=s_plane[:], start=True, stop=True)
        qv_bf = keep.tile([P, Q, PACK], BF16, tag="then_f1", align_bytes=64)
        nc.vector.tensor_copy(out=qv_bf[:, :, 0:2], in_=qv_ps[0][:, : 2 * Q].rearrange("p (t q) -> p q t", t=2))
        nc.scalar.copy(out=qv_bf[:, :, 2:4], in_=qv_ps[1][:, : 2 * Q].rearrange("p (t q) -> p q t", t=2))

        q_codes = keep.tile([P, Q], U32, align_bytes=64)
        q_plane = keep.tile([P, Q], U8, align_bytes=64)
        nc.vector.quantize_mx(out=q_codes[:].bitcast(FP8X4), scales=q_plane[:], in_=qv_bf[:].rearrange("p q t -> p (q t)"))

        f1 = keep.tile([P, T], F32, tag="then_f1", align_bytes=64)
        nc.vector.memset(f1[:], 0.0)
        b_sb = keep.tile([P, T], F32, tag="scores")
        lo = 0
        for j, width in enumerate((512, 256, 128, 128)):
            bank = psum.tile([P, BANK], F32, name="b_%d" % j, tag="b_%d" % j)
            nc.tensor.matmul_mx(out=bank[:, :width], lhsT=q_codes[:].bitcast(FP8X4), lhsT_scale=q_plane[:],
                                rhs=draft_sb[:, 4 * lo : 4 * (lo + width)].bitcast(FP8X4), rhs_scale=draft_plane[:, lo : lo + width],
                                start=True, stop=True)
            if j % 2 == 0:
                nc.scalar.copy(out=b_sb[:, lo : lo + width], in_=bank[:, :width])
            else:
                nc.vector.tensor_copy(out=b_sb[:, lo : lo + width], in_=bank[:, :width])
            lo = lo + width

        gb = keep.tile([P, I], F32)
        nc.vector.tensor_copy(gb[:, :HALF], b_sb[:].indirect(list2[:, : HALF // 16]))
        nc.scalar.activation(gb[:, HALF:], b_sb[:].indirect(list2[:, HALF // 16 :]), COPY)
        nc.scalar.activation(f2[:].indirect(list4[:]), gb[:], COPY)

        a_sb = keep.tile([P, T], F32, tag="scores")
        for h in range(2):
            bank = psum.tile([P, BANK], F32, name="a_%d" % h, tag="first_%d" % h)
            nc.tensor.matmul_mx(out=bank[:], lhsT=q_codes[:].bitcast(FP8X4), lhsT_scale=q_plane[:],
                                rhs=cache_sb[:, 2 * BANK * h : 2 * BANK * (h + 1)].bitcast(FP4X4), rhs_scale=cache_plane[:, BANK * h : BANK * (h + 1)],
                                start=True, stop=True)
            nc.vector.tensor_copy(out=a_sb[:, BANK * h : BANK * (h + 1)], in_=bank[:])
        ga = keep.tile([P, I], F32, tag="then_late")
        w = keep.tile([P, I], F32)
        for h in range(2):
            nc.vector.tensor_copy(ga[:, HALF * h : HALF * (h + 1)], a_sb[:].indirect(list1[:, HALF // 16 * h : HALF // 16 * (h + 1)]))
        for h in range(2):
            cols = slice(HALF * h, HALF * (h + 1))
            nc.vector.tensor_tensor(w[:, cols], ga[:, cols], gb[:, cols], ALU.min)
        f1_late = keep.tile([P, T], F32, tag="then_late")
        nc.vector.memset(f1_late[:], 0.0)
        nc.scalar.activation(f1[:].indirect(list3[:, : HALF // 16]), w[:, :HALF], COPY)
        nc.scalar.activation(f1_late[:].indirect(list3[:, HALF // 16 :]), w[:, HALF:], COPY)
        r_early = keep.tile([P, T], F32)
        nc.vector.tensor_tensor(r_early[:], f1[:], f2[:], ALU.subtract)

        c0_ps = []
        for h in range(2):
            bank = psum.tile([P, BANK], F32, name="c0_%d" % h, tag="b_%d" % h)
            nc.tensor.matmul_mx(out=bank[:], lhsT=s_codes[:].bitcast(FP8X4), lhsT_scale=s_plane[:],
                                rhs=arch_sb[:, 2 * BANK * h : 2 * BANK * (h + 1)].bitcast(FP4X4), rhs_scale=arch_plane[:, BANK * h : BANK * (h + 1)],
                                start=True, stop=True)
            c0_ps.append(bank)

        r = keep.tile([P, T], F32)
        cc = keep.tile([P, T], F32)
        for h in range(2):
            cols = slice(BANK * h, BANK * (h + 1))
            nc.vector.tensor_tensor(r[:, cols], f1_late[:, cols], r_early[:, cols], ALU.add)
        for h in range(2):
            cols = slice(BANK * h, BANK * (h + 1))
            nc.vector.tensor_tensor(cc[:, cols], c0_ps[h][:], r[:, cols], ALU.max)

        y0 = keep.tile([P, HALF], F32, align_bytes=256)
        y1 = keep.tile([P, HALF], F32, align_bytes=256)
        gc = keep.tile([P, HALF], F32)
        nc.vector.tensor_tensor(y0[:], cc[:].indirect(list5[:, : HALF // 16]), w[:, :HALF], ALU.subtract)
        nc.scalar.activation(gc[:], cc[:].indirect(list5[:, HALF // 16 :]), COPY)
        nc.sync.dma_start(out=out[:, :HALF], in_=y0[:])
        for j, queue in enumerate((nc.scalar, nc.sync)):
            cols = slice(HALF // 2 * j, HALF // 2 * (j + 1))
            nc.vector.tensor_tensor(y1[:, cols], gc[:, cols], w[:, HALF:][:, cols], ALU.subtract)
            queue.dma_start(out=out[:, HALF:][:, cols], in_=y1[:, cols])
